import numpy as np
import ml_dtypes


def mxq(x, axis, fmt="e4m3"):
    dtype, down = {"e4m3": (ml_dtypes.float8_e4m3fn, 7), "e5m2": (ml_dtypes.float8_e5m2, 14)}[fmt]
    v = np.moveaxis(np.asarray(x, np.float32).astype(ml_dtypes.bfloat16).astype(np.float64), axis, -1)
    blocks = v.reshape(v.shape[:-1] + (-1, 32))
    amax = np.abs(blocks).max(-1, keepdims=True)
    byte = np.maximum(np.where(amax > 0, np.frexp(amax)[1] - 1 + 127, 0) - down, 1)
    scale = np.exp2(byte - 127.0)
    codes = (blocks / scale).astype(np.float32).astype(dtype).astype(np.float64)
    return np.moveaxis((codes * scale).reshape(v.shape), -1, axis)


WIDE = False


def mx_kscale(k):
    if not WIDE:
        return np.ones(k)
    levels = np.array([10, -10, 5, -5, 0])
    if k % 512:
        return np.exp2(np.random.permutation(np.resize(levels, k // 32))).repeat(32)
    a = np.empty((k // 512, 16))
    for p in range(k // 512):
        a[p, :8] = np.random.permutation(np.resize(levels, 8))
        for g in range(8):
            far = levels[np.abs(levels - a[p, g]) >= 10]
            a[p, g + 8] = far[np.random.randint(len(far))]
    return np.exp2(a.ravel()).repeat(32)


BF16 = ml_dtypes.bfloat16


def bf(x):
    return np.asarray(x, np.float32).astype(BF16)


def f64(x):
    return np.asarray(x).astype(np.float64)


N, D, H, O = 4096, 512, 256, 1024
DAMP = 0.2


def draw0():
    u = mx_kscale(O)
    t = mx_kscale(N)
    return {
        "x": bf(np.random.standard_normal((N, D))),
        "a": bf(np.random.standard_normal((N, H))),
        "g": bf(np.random.standard_normal((N, O)) * u[None, :]),
        "w2": bf(np.random.standard_normal((H, O)) / np.sqrt(O) / u[None, :]),
        "p": bf(np.random.uniform(0.5, 1.5, N) * t),
        "q": bf(np.random.uniform(0.5, 1.5, N) / t),
        "s": bf(np.random.standard_normal(N)),
    }


def backprop_delta(a, g, w2):
    back = mxq(g, 1, "e4m3") @ mxq(w2, 1, "e4m3").T
    return back * (1.0 - np.tanh(a) ** 2)


def core(x, a, g, w2, p, q, s):
    x, a, g, w2, p, q, s = f64(x), f64(a), f64(g), f64(w2), f64(p), f64(q), f64(s)
    n = x.shape[0]

    d = backprop_delta(a, g, w2)

    xp = x * p[:, None]
    dq = d * q[:, None]
    grad = (mxq(xp, 0, "e4m3").T @ mxq(dq, 0, "e4m3")) / np.sqrt(n)

    x2 = x * xp * s[:, None]
    d2 = d * dq * s[:, None]
    fisher = (mxq(x2, 0, "e4m3").T @ mxq(d2, 0, "e4m3")) / n

    return grad / (fisher + DAMP)


def e4m3fn_bytes(y):
    return np.clip(np.asarray(y, np.float64), -448.0, 448.0).astype(np.float32).astype(ml_dtypes.float8_e4m3fn).view(np.uint8)


def e4m3fn_values(b):
    return np.asarray(b, np.uint8).view(ml_dtypes.float8_e4m3fn).astype(np.float64)


def setup_inputs():
    d = draw0()
    x0 = np.asarray(d['g']).astype(np.float64)
    s = (np.max(np.abs(x0), axis=(0,), keepdims=True) / 448.0).astype(np.float32)
    out = {}
    for k, v in d.items():
        if k == 'g':
            out['g_bytes'] = e4m3fn_bytes(x0 / s.astype(np.float64))
            out['g_scale'] = s
        else:
            out[k] = v
    return out


def reference(x, a, g_bytes, g_scale, w2, p, q, s):
    return core(x, a, e4m3fn_values(g_bytes) * g_scale.astype(np.float64), w2, p, q, s)

@@ -1,0 +1,399 @@
+from contextlib import ExitStack
+
+import concourse.mybir as mybir
+from concourse.masks import make_identity
+
+N, D, H, O = 4096, 512, 256, 1024
+FLOPS = 2 * N * O * H + 2 * (2 * N * D * H)
+
+F32 = mybir.dt.float32
+BF16 = mybir.dt.bfloat16
+U32 = mybir.dt.uint32
+U8 = mybir.dt.uint8
+FP8 = mybir.dt.float8_e4m3fn
+FP8X4 = mybir.dt.float8_e4m3fn_x4
+ACT = mybir.ActivationFunctionType
+ALU = mybir.AluOpType
+
+P = 128
+T = 4
+GROUP = P * T
+GROUPS = N // GROUP
+KP = O // GROUP
+ID2 = "A"
+
+
+def tile_diagonalfishernaturalgradient_t_kernel(tc, x, a, g_bytes, g_scale, w2, p, q, s, out):
+    nc = tc.nc
+    with ExitStack() as ctx:
+        keep = ctx.enter_context(tc.tile_pool(name="keep", bufs=1))
+        loads = ctx.enter_context(tc.tile_pool(name="loads", bufs=4))
+        work = ctx.enter_context(tc.tile_pool(name="work", bufs=2))
+        psum = ctx.enter_context(tc.psum_pool(name="psum", bufs=1))
+        ctx.enter_context(tc.manual_schedule())
+
+        V, A, PO, PE = nc.vector, nc.scalar, nc.gpsimd, nc.tensor
+
+        warm = keep.tile([P, 1], F32, name="warm")
+        V.memset(warm[:], 1.0)
+        warm2 = keep.tile([P, 1], F32, name="warm2")
+        A.activation(out=warm2[:], in_=warm[:], func=ACT.Abs_reciprocal_sqrt)
+        gain = keep.tile([P, 3, GROUPS * T], BF16, name="gain")
+        scale4 = keep.tile([P, KP, T], F32, name="scale4")
+        A.dma_start(out=scale4[:], in_=g_scale.rearrange("o (g p t) -> p (o g) t", p=P, t=T))
+        for i, v in enumerate((p, s, q)):
+            A.dma_start(out=gain[:, i, :].rearrange("p (g t) -> p g t", t=T), in_=v.rearrange("(g p t) -> p g t", p=P, t=T))
+        gb, xs, as_ = {}, {}, {}
+        xv = x.rearrange("(g p t) d -> g p (t d)", p=P, t=T)
+        av = a.rearrange("(g p t) h -> g p (t h)", p=P, t=T)
+        gv = g_bytes.rearrange("(g p t) o -> g p (t o)", p=P, t=T)
+        w2s = keep.tile([P, 2, O], BF16, name="w2s")
+
+        def load(G):
+            g_t = loads.tile([P, T * O], U8, name="g_t")
+            x_t = loads.tile([P, T, D], BF16, name="x_t")
+            a_t = loads.tile([P, T * H], BF16, name="a_t")
+            if G == 0:
+                nc.sync.dma_start(out=g_t[:, : 2 * O], in_=gv[G][:, : 2 * O])
+                nc.sync.dma_start(out=g_t[:, 2 * O :], in_=gv[G][:, 2 * O :])
+            else:
+                nc.sync.dma_start(out=g_t[:], in_=gv[G])
+            nc.sync.dma_start(out=x_t[:].rearrange("p t d -> p (t d)"), in_=xv[G])
+            if G == 0:
+                nc.sync.dma_start(out=w2s[:], in_=w2.rearrange("(i r) o -> r i o", r=P))
+            nc.sync.dma_start(out=a_t[:], in_=av[G])
+            gb[G], xs[G], as_[G] = g_t, x_t, a_t
+
+        ident = keep.tile([P, P], F32, name="ident")
+        make_identity(nc, ident[:])
+        for G in range(4):
+            load(G)
+
+        gc, gT, gq, bk, sqd, nds, d2ps, dis, dcs, xpps, x2ps, xis, xcs, trs = ({} for _ in range(14))
+        grad, fish = [], []
+        for hh in range(2):
+            g_acc = psum.tile([P, D], F32, name="grad%d" % hh)
+            f_acc = psum.tile([P, D], F32, name="fish%d" % hh)
+            grad.append(g_acc)
+            fish.append(f_acc)
+
+        def cast(G, t, eng):
+            if G not in gc:
+                c = work.tile([P, T, O], BF16, name="gc", bufs=3)
+                gc[G] = c
+            src = gb[G][:, t * O : (t + 1) * O].bitcast(FP8)
+            if eng == "V":
+                V.tensor_copy(out=gc[G][:, t, :], in_=src)
+            else:
+                A.copy(out=gc[G][:, t, :], in_=src)
+
+        def words_to_bank(words, starts):
+            xt = psum.tile([P, 2, 2 * P], F32, name="xt", bufs=2)
+            for i in range(2):
+                for u in range(2):
+                    PE.transpose(xt[:, u, i * P : (i + 1) * P], words[:, starts[i] + u : starts[i] + 256 : 2], ident[:])
+            return xt
+
+        def tr(G, b):
+            g2, tp = b // 2, b % 2
+            words = gc[G][:].rearrange("p t k -> p (t k)").bitcast(F32)
+            trs[G, b] = words_to_bank(words, [512 * (2 * tp + i) + 256 * g2 for i in range(2)])
+
+        def ep(G, b):
+            g2, tp = b // 2, b % 2
+            if b == 0:
+                gT_t = work.tile([P, KP, T * P * T], BF16, name="gT", align_bytes=64)
+                gT[G] = gT_t
+            V.tensor_tensor(
+                out=gT[G][:, g2, tp * 1024 : (tp + 1) * 1024].rearrange("p (r u e) -> p r u e", u=2, e=2),
+                in0=trs[G, b][:].bitcast(BF16).rearrange("p u (r e) -> p r u e", e=2),
+                in1=scale4[:, g2 : g2 + 1, :].to_broadcast([P, 256, T]).rearrange("p r (u e) -> p r u e", e=2),
+                op=ALU.mult,
+            )
+
+        def q_g(G, g2):
+            if g2 == 0:
+                codes = work.tile([P, KP, T * P], U32, name="gcodes", align_bytes=64)
+                planes = work.tile([P, KP, T * P], U8, name="gplanes", align_bytes=64)
+                gq[G] = (codes, planes)
+            codes, planes = gq[G]
+            V.quantize_mx(out=codes[:, g2, :].bitcast(FP8X4), scales=planes[:, g2, :], in_=gT[G][:, g2, :])
+
+        HT = H // 2
+
+        def s1(G):
+            codes, planes = gq[G]
+            for hh in range(2):
+                b = psum.tile([P, T, HT], F32, name="bk%d" % hh)
+                bk[G, hh] = b
+                for t in range(T):
+                    for g2 in range(KP):
+                        PE.matmul_mx(
+                            out=b[:, t, :],
+                            lhsT=codes[:, g2, t * P : (t + 1) * P].bitcast(FP8X4),
+                            lhsT_scale=planes[:, g2, t * P : (t + 1) * P],
+                            rhs=w2c[:, g2, hh * HT : (hh + 1) * HT].bitcast(FP8X4),
+                            rhs_scale=w2p[:, g2, hh * HT : (hh + 1) * HT],
+                            start=(g2 == 0),
+                            stop=(g2 == KP - 1),
+                        )
+
+        def tanh2(G):
+            th = work.tile([P, T * H], F32, name="th")
+            sq = work.tile([P, T, H], F32, name="sq")
+            A.activation(out=th[:], in_=as_[G][:], func=ACT.Tanh)
+            A.activation(out=sq[:].rearrange("p t h -> p (t h)"), in_=th[:], func=ACT.Square)
+            sqd[G] = sq
+
+        def nd(G, hh):
+            if hh == 0:
+                n_t = work.tile([P, T, H], F32, name="nd")
+                nds[G] = n_t
+            c = slice(hh * HT, (hh + 1) * HT)
+            V.scalar_tensor_tensor(
+                out=nds[G][:, :, c], in0=sqd[G][:, :, c], scalar=1.0, in1=bk[G, hh][:], op0=ALU.subtract, op1=ALU.mult
+            )
+
+        def dq(G, h0, h1):
+            if h0 == 0:
+                d_i = work.tile([P, 2, 2, HT, T], BF16, name="d_i", align_bytes=64)
+                dis[G] = d_i
+            n = h1 - h0
+            V.tensor_tensor(
+                out=dis[G][:, h0:h1, 0, :, :],
+                in0=nds[G][:, :, h0 * HT : h1 * HT].rearrange("p t (c h) -> p c h t", h=HT),
+                in1=negq[:, G * T : (G + 1) * T].rearrange("p (b c t) -> p b c t", b=1, c=1).to_broadcast([P, n, HT, T]),
+                op=ALU.mult,
+            )
+
+        def d2p(G, h0, h1):
+            if h0 == 0:
+                pl = work.tile([P, T, H], BF16, name="d2p")
+                d2ps[G] = pl
+            c = slice(h0 * HT, h1 * HT)
+            for t in range(T):
+                A.activation(
+                    out=d2ps[G][:, t, c], in_=nds[G][:, t, c], func=ACT.Square, scale=root[:, 1, G * T + t : G * T + t + 1]
+                )
+
+        def i_d2(G, h0, h1, eng):
+            src = d2ps[G][:, :, h0 * HT : h1 * HT].rearrange("p t (c h) -> p c h t", h=HT)
+            dst = dis[G][:, h0:h1, 1, :, :]
+            if eng == "V":
+                V.tensor_copy(out=dst, in_=src)
+            else:
+                A.copy(out=dst, in_=src)
+
+        def q_d(G, h0, h1):
+            if h0 == 0:
+                codes = work.tile([P, 2 * H], U32, name="dcodes", align_bytes=64)
+                planes = work.tile([P, 2 * H], U8, name="dplanes", align_bytes=64)
+                dcs[G] = (codes, planes)
+            codes, planes = dcs[G]
+            c = slice(h0 * 2 * HT, h1 * 2 * HT)
+            V.quantize_mx(
+                out=codes[:, c].bitcast(FP8X4), scales=planes[:, c], in_=dis[G][:, h0:h1].rearrange("p c w h t -> p (c w h t)")
+            )
+
+        def xp(G):
+            pl = work.tile([P, T, D], BF16, name="xpp")
+            xpps[G] = pl
+            for t in range(T):
+                V.tensor_scalar(out=pl[:, t, :], in0=xs[G][:, t, :], scalar1=g32[:, 0, G * T + t : G * T + t + 1], scalar2=None, op0=ALU.mult)
+
+        def x2(G):
+            pl = work.tile([P, T, D], BF16, name="x2p")
+            x2ps[G] = pl
+            for t in range(T):
+                A.activation(out=pl[:, t, :], in_=xs[G][:, t, :], func=ACT.Square, scale=root[:, 0, G * T + t : G * T + t + 1])
+
+        def i_x(G, which, part, eng):
+            if which == 0 and part == 0:
+                x_i = work.tile([P, 2, D, T], BF16, name="x_i", align_bytes=64)
+                xis[G] = x_i
+            c = slice(part * D // 2, (part + 1) * D // 2)
+            src = (xpps, x2ps)[which][G][:, :, c].rearrange("p t d -> p d t")
+            dst = xis[G][:, which, c, :]
+            if eng == "P":
+                PO.tensor_scalar(out=dst, in0=src, scalar1=1.0, scalar2=0.0, op0=ALU.mult, op1=ALU.add)
+            elif eng == "V":
+                V.tensor_copy(out=dst, in_=src)
+            else:
+                A.copy(out=dst, in_=src)
+
+        def q_x(G):
+            codes = work.tile([P, 2 * D], U32, name="xcodes", align_bytes=64, bufs=3)
+            planes = work.tile([P, 2 * D], U8, name="xplanes", align_bytes=64, bufs=3)
+            V.quantize_mx(out=codes[:].bitcast(FP8X4), scales=planes[:], in_=xis[G][:].rearrange("p w d t -> p (w d t)"))
+            xcs[G] = (codes, planes)
+
+        def s2(G, h0, h1):
+            dc, dp = dcs[G]
+            xc, xpl = xcs[G]
+            for acc, w in ((fish, 1), (grad, 0)):
+                for hh in range(h0, h1):
+                    c0 = (2 * hh + w) * HT
+                    PE.matmul_mx(
+                        out=acc[hh][:],
+                        lhsT=dc[:, c0 : c0 + P].bitcast(FP8X4),
+                        lhsT_scale=dp[:, c0 : c0 + P],
+                        rhs=xc[:, w * D : (w + 1) * D].bitcast(FP8X4),
+                        rhs_scale=xpl[:, w * D : (w + 1) * D],
+                        start=(G == 0),
+                        stop=(G == GROUPS - 1),
+                    )
+
+        cast(0, 0, "V")
+        cast(0, 1, "A")
+        tr(0, 0)
+        cast(0, 2, "V")
+        cast(0, 3, "A")
+        tr(0, 1)
+        NS = GROUPS * T
+        g32 = keep.tile([P, 3, NS], F32, name="g32")
+        negq = keep.tile([P, NS], F32, name="negq")
+        prod = keep.tile([P, 2, NS], F32, name="prod")
+        mag = keep.tile([P, 2, NS], F32, name="mag")
+        r0 = keep.tile([P, 2, NS], F32, name="r0")
+        w0 = keep.tile([P, 2, NS], F32, name="w0")
+        z0 = keep.tile([P, 2, NS], F32, name="z0")
+        k0 = keep.tile([P, 2, NS], F32, name="k0")
+        root = keep.tile([P, 2, NS], F32, name="root")
+        V.tensor_copy(out=g32[:], in_=gain[:])
+        V.tensor_scalar(out=negq[:], in0=gain[:, 2, :], scalar1=-1.0, scalar2=None, op0=ALU.mult)
+        V.tensor_tensor(out=prod[:, 0, :], in0=g32[:, 0, :], in1=g32[:, 1, :], op=ALU.mult)
+        V.tensor_tensor(out=prod[:, 1, :], in0=g32[:, 2, :], in1=g32[:, 1, :], op=ALU.mult)
+        V.scalar_tensor_tensor(out=mag[:], in0=prod[:], scalar=-1.0, in1=prod[:], op0=ALU.mult, op1=ALU.max)
+        V.tensor_scalar(out=w0[:], in0=mag[:], scalar1=1e-30, scalar2=None, op0=ALU.max)
+        A.activation(out=r0[:], in_=w0[:], func=ACT.Abs_reciprocal_sqrt)
+        xp(0)
+        for part in range(2):
+            i_x(0, 0, part, "P")
+        ep(0, 0)
+        w1 = keep.tile([P, 2, NS], F32, name="w1")
+        V.tensor_tensor(out=w1[:], in0=mag[:], in1=r0[:], op=ALU.mult)
+        tr(0, 2)
+        ep(0, 1)
+        V.tensor_tensor(out=z0[:], in0=w1[:], in1=r0[:], op=ALU.mult)
+        tr(0, 3)
+        ep(0, 2)
+        V.tensor_scalar(out=k0[:], in0=z0[:], scalar1=-0.5, scalar2=1.5, op0=ALU.mult, op1=ALU.add)
+        q_g(0, 0)
+        V.tensor_tensor(out=root[:], in0=w1[:], in1=k0[:], op=ALU.mult)
+        w2T = keep.tile([P, KP, H * T], BF16, name="w2T", align_bytes=64)
+        w2c = keep.tile([P, KP, H], U32, name="w2c", align_bytes=64)
+        w2p = keep.tile([P, KP, H], U8, name="w2p", align_bytes=64)
+        w2words = w2s[:].rearrange("p i o -> p (i o)").bitcast(F32)
+        wt = [None, None]
+        wt[0] = words_to_bank(w2words, [512 * r for r in range(2)])
+        ep(0, 3)
+        wt[1] = words_to_bank(w2words, [512 * r + 256 for r in range(2)])
+        for t in range(T):
+            cast(1, t, "A")
+        for g2 in range(KP):
+            V.tensor_copy(
+                out=w2T[:, g2, :].bitcast(F32).rearrange("p (r u) -> p r u", u=2), in_=wt[g2][:].rearrange("p u r -> p r u")
+            )
+        q_g(0, 1)
+        V.quantize_mx(
+            out=w2c[:].rearrange("p g h -> p (g h)").bitcast(FP8X4),
+            scales=w2p[:].rearrange("p g h -> p (g h)"),
+            in_=w2T[:].rearrange("p g c -> p (g c)"),
+        )
+        x2(0)
+        tanh2(0)
+        tr(1, 0)
+        tr(1, 1)
+        s1(0)
+        xp(1)
+        for part in range(2):
+            i_x(0, 1, part, "P")
+        x2(1)
+        for t in range(T):
+            cast(2, t, "A")
+
+        for G in range(1, GROUPS):
+            L = G - 1
+            for part in range(2):
+                i_x(G, 0, part, "P")
+            ep(G, 0)
+            tr(G, 2)
+            ep(G, 1)
+            tr(G, 3)
+            nd(L, 0)
+            nd(L, 1)
+            d2p(L, 0, 2)
+            ep(G, 2)
+            for part in range(2):
+                i_x(G, 1, part, "P")
+            tanh2(G)
+            ep(G, 3)
+            if G + 1 < GROUPS:
+                tr(G + 1, 0)
+                tr(G + 1, 1)
+            dq(L, 0, 2)
+            i_d2(L, 0, 2, ID2)
+            q_g(G, 0)
+            if L == 0:
+                q_x(0)
+            q_g(G, 1)
+            s1(G)
+            if G + 2 < GROUPS:
+                for t in range(T):
+                    cast(G + 2, t, "A")
+            if G + 3 < GROUPS:
+                load(G + 3)
+            if G + 1 < GROUPS:
+                xp(G + 1)
+                x2(G + 1)
+            q_d(L, 0, 2)
+            q_x(G)
+            s2(L, 0, 2)
+
+        ot = keep.tile([P, 4, H], F32, name="ot")
+        ov = out.rearrange("(t p) h -> p t h", p=P)
+        L = GROUPS - 1
+        rr, o1, o2 = {}, {}, {}
+        warm3 = keep.tile([P, 1], F32, name="warm3")
+
+        def tail_d(hh):
+            nd(L, hh)
+            d2p(L, hh, hh + 1)
+            dq(L, hh, hh + 1)
+
+        def ratio(hh, c0, c1):
+            n = c1 - c0
+            r_t = work.tile([P, n], F32, name="rr")
+            o1_t = work.tile([P, n], F32, name="o1")
+            o2_t = work.tile([P, n], F32, name="o2")
+            A.activation(out=r_t[:], in_=fish[hh][:, c0:c1], func=ACT.Abs_reciprocal_sqrt, scale=1.0 / N, bias=0.2)
+            V.scalar_tensor_tensor(out=o1_t[:], in0=grad[hh][:, c0:c1], scalar=1.0 / 64.0, in1=r_t[:], op0=ALU.mult, op1=ALU.mult)
+            V.tensor_tensor(out=o2_t[:], in0=o1_t[:], in1=r_t[:], op=ALU.mult)
+            return o2_t
+
+        def turn(hh, c0, c1, o2_t):
+            m = (c1 - c0) // P
+            xt = psum.tile([P, m, P], F32, name="xt", bufs=2)
+            for d in range(m):
+                PE.transpose(xt[:, d, :], o2_t[:, d * P : (d + 1) * P], ident[:])
+            dst = ot[:, c0 // P : c1 // P, hh * P : (hh + 1) * P]
+            A.copy(out=dst, in_=xt[:])
+            nc.sync.dma_start(out=ov[:, c0 // P : c1 // P, hh * P : (hh + 1) * P], in_=dst)
+
+        tail_d(0)
+        tail_d(1)
+        i_d2(L, 0, 1, "V")
+        i_d2(L, 1, 2, "V")
+        q_d(L, 0, 1)
+        s2(L, 0, 1)
+        q_d(L, 1, 2)
+        s2(L, 1, 2)
+        A.activation(out=warm3[:], in_=warm[:], func=ACT.Abs_reciprocal_sqrt)
+        parts = [(hh, c0) for hh in range(2) for c0 in (0, 256)]
+        pend = None
+        for hh, c0 in parts:
+            o = ratio(hh, c0, c0 + 256)
+            if pend is not None:
+                turn(*pend)
+            pend = (hh, c0, c0 + 256, o)
+        turn(*pend)

@@ -20,7 +20,10 @@ T = 4
 GROUP = P * T
 GROUPS = N // GROUP
 KP = O // GROUP
-ID2 = "A"
+
+
+HT = H // 2
+OPT = {"id2": [("P", 0, 128), ("A", 128, 256)]}
 
 
 def tile_diagonalfishernaturalgradient_t_kernel(tc, x, a, g_bytes, g_scale, w2, p, q, s, out):
@@ -56,11 +59,10 @@ def tile_diagonalfishernaturalgradient_t_kernel(tc, x, a, g_bytes, g_scale, w2, 
             if G == 0:
                 nc.sync.dma_start(out=g_t[:, : 2 * O], in_=gv[G][:, : 2 * O])
                 nc.sync.dma_start(out=g_t[:, 2 * O :], in_=gv[G][:, 2 * O :])
+                nc.sync.dma_start(out=w2s[:], in_=w2.rearrange("(i r) o -> r i o", r=P))
             else:
                 nc.sync.dma_start(out=g_t[:], in_=gv[G])
             nc.sync.dma_start(out=x_t[:].rearrange("p t d -> p (t d)"), in_=xv[G])
-            if G == 0:
-                nc.sync.dma_start(out=w2s[:], in_=w2.rearrange("(i r) o -> r i o", r=P))
             nc.sync.dma_start(out=a_t[:], in_=av[G])
             gb[G], xs[G], as_[G] = g_t, x_t, a_t
 
@@ -76,6 +78,19 @@ def tile_diagonalfishernaturalgradient_t_kernel(tc, x, a, g_bytes, g_scale, w2, 
             f_acc = psum.tile([P, D], F32, name="fish%d" % hh)
             grad.append(g_acc)
             fish.append(f_acc)
+
+        def blocks(G):
+            return [(0, H)] if G < GROUPS - 1 else [(0, HT), (HT, H)]
+
+        def interleave(dst, src, eng):
+            d4 = dst.rearrange("p (c i) t -> p c t i", i=4)
+            s4 = src.rearrange("p t (c i) -> p c t i", i=4)
+            if eng == "P":
+                PO.tensor_scalar(out=d4, in0=s4, scalar1=1.0, scalar2=0.0, op0=ALU.mult, op1=ALU.add)
+            elif eng == "V":
+                V.tensor_copy(out=d4, in_=s4)
+            else:
+                A.copy(out=d4, in_=s4)
 
         def cast(G, t, eng):
             if G not in gc:
@@ -119,24 +134,29 @@ def tile_diagonalfishernaturalgradient_t_kernel(tc, x, a, g_bytes, g_scale, w2, 
             codes, planes = gq[G]
             V.quantize_mx(out=codes[:, g2, :].bitcast(FP8X4), scales=planes[:, g2, :], in_=gT[G][:, g2, :])
 
-        HT = H // 2
-
         def s1(G):
             codes, planes = gq[G]
-            for hh in range(2):
-                b = psum.tile([P, T, HT], F32, name="bk%d" % hh)
-                bk[G, hh] = b
-                for t in range(T):
-                    for g2 in range(KP):
-                        PE.matmul_mx(
-                            out=b[:, t, :],
-                            lhsT=codes[:, g2, t * P : (t + 1) * P].bitcast(FP8X4),
-                            lhsT_scale=planes[:, g2, t * P : (t + 1) * P],
-                            rhs=w2c[:, g2, hh * HT : (hh + 1) * HT].bitcast(FP8X4),
-                            rhs_scale=w2p[:, g2, hh * HT : (hh + 1) * HT],
-                            start=(g2 == 0),
-                            stop=(g2 == KP - 1),
-                        )
+            n = 0
+            for blk in blocks(G):
+                w = blk[1] - blk[0]
+                nt = 512 // w
+                bk[G, blk] = []
+                for t0 in range(0, T, nt):
+                    b = psum.tile([P, nt, w], F32, name="bk%d" % n)
+                    n += 1
+                    bk[G, blk].append((t0, nt, b))
+                    for i in range(nt):
+                        c = slice((t0 + i) * P, (t0 + i + 1) * P)
+                        for g2 in range(KP):
+                            PE.matmul_mx(
+                                out=b[:, i, :],
+                                lhsT=codes[:, g2, c].bitcast(FP8X4),
+                                lhsT_scale=planes[:, g2, c],
+                                rhs=w2c[:, g2, blk[0] : blk[1]].bitcast(FP8X4),
+                                rhs_scale=w2p[:, g2, blk[0] : blk[1]],
+                                start=(g2 == 0),
+                                stop=(g2 == KP - 1),
+                            )
 
         def tanh2(G):
             th = work.tile([P, T * H], F32, name="th")
@@ -145,61 +165,56 @@ def tile_diagonalfishernaturalgradient_t_kernel(tc, x, a, g_bytes, g_scale, w2, 
             A.activation(out=sq[:].rearrange("p t h -> p (t h)"), in_=th[:], func=ACT.Square)
             sqd[G] = sq
 
-        def nd(G, hh):
-            if hh == 0:
-                n_t = work.tile([P, T, H], F32, name="nd")
-                nds[G] = n_t
-            c = slice(hh * HT, (hh + 1) * HT)
-            V.scalar_tensor_tensor(
-                out=nds[G][:, :, c], in0=sqd[G][:, :, c], scalar=1.0, in1=bk[G, hh][:], op0=ALU.subtract, op1=ALU.mult
-            )
+        def nd(G, blk):
+            w = blk[1] - blk[0]
+            n_t = work.tile([P, T, w], F32, name="nd%d" % w)
+            nds[G, blk] = n_t
+            for t0, nt, b in bk[G, blk]:
+                V.scalar_tensor_tensor(
+                    out=n_t[:, t0 : t0 + nt, :],
+                    in0=sqd[G][:, t0 : t0 + nt, blk[0] : blk[1]],
+                    scalar=1.0,
+                    in1=b[:],
+                    op0=ALU.subtract,
+                    op1=ALU.mult,
+                )
 
-        def dq(G, h0, h1):
-            if h0 == 0:
-                d_i = work.tile([P, 2, 2, HT, T], BF16, name="d_i", align_bytes=64)
-                dis[G] = d_i
-            n = h1 - h0
+        def d_tile(G, blk):
+            w = blk[1] - blk[0]
+            d_i = work.tile([P, 2, w, T], BF16, name="d_i%d" % w, align_bytes=64)
+            dis[G, blk] = d_i
+
+        def dq(G, blk):
+            w = blk[1] - blk[0]
             V.tensor_tensor(
-                out=dis[G][:, h0:h1, 0, :, :],
-                in0=nds[G][:, :, h0 * HT : h1 * HT].rearrange("p t (c h) -> p c h t", h=HT),
-                in1=negq[:, G * T : (G + 1) * T].rearrange("p (b c t) -> p b c t", b=1, c=1).to_broadcast([P, n, HT, T]),
+                out=dis[G, blk][:, 0],
+                in0=nds[G, blk][:].rearrange("p t h -> p h t"),
+                in1=negq[:, G * T : (G + 1) * T].rearrange("p (b t) -> p b t", b=1).to_broadcast([P, w, T]),
                 op=ALU.mult,
             )
 
-        def d2p(G, h0, h1):
-            if h0 == 0:
-                pl = work.tile([P, T, H], BF16, name="d2p")
-                d2ps[G] = pl
-            c = slice(h0 * HT, h1 * HT)
+        def d2p(G, blk):
+            w = blk[1] - blk[0]
+            pl = work.tile([P, T, w], BF16, name="d2p%d" % w)
+            d2ps[G, blk] = pl
             for t in range(T):
-                A.activation(
-                    out=d2ps[G][:, t, c], in_=nds[G][:, t, c], func=ACT.Square, scale=root[:, 1, G * T + t : G * T + t + 1]
-                )
+                A.activation(out=pl[:, t, :], in_=nds[G, blk][:, t, :], func=ACT.Square, scale=root[:, 1, G * T + t : G * T + t + 1])
 
-        def i_d2(G, h0, h1, eng):
-            src = d2ps[G][:, :, h0 * HT : h1 * HT].rearrange("p t (c h) -> p c h t", h=HT)
-            dst = dis[G][:, h0:h1, 1, :, :]
-            if eng == "V":
-                V.tensor_copy(out=dst, in_=src)
-            else:
-                A.copy(out=dst, in_=src)
+        def i_d2(G, blk, eng, h0, h1):
+            interleave(dis[G, blk][:, 1, h0:h1, :], d2ps[G, blk][:, :, h0:h1], eng)
 
-        def q_d(G, h0, h1):
-            if h0 == 0:
-                codes = work.tile([P, 2 * H], U32, name="dcodes", align_bytes=64)
-                planes = work.tile([P, 2 * H], U8, name="dplanes", align_bytes=64)
-                dcs[G] = (codes, planes)
-            codes, planes = dcs[G]
-            c = slice(h0 * 2 * HT, h1 * 2 * HT)
-            V.quantize_mx(
-                out=codes[:, c].bitcast(FP8X4), scales=planes[:, c], in_=dis[G][:, h0:h1].rearrange("p c w h t -> p (c w h t)")
-            )
+        def q_d(G, blk):
+            w = blk[1] - blk[0]
+            codes = work.tile([P, 2 * w], U32, name="dcodes%d" % w, align_bytes=64)
+            planes = work.tile([P, 2 * w], U8, name="dplanes%d" % w, align_bytes=64)
+            dcs[G, blk] = (codes, planes)
+            V.quantize_mx(out=codes[:].bitcast(FP8X4), scales=planes[:], in_=dis[G, blk][:].rearrange("p w h t -> p (w h t)"))
 
         def xp(G):
             pl = work.tile([P, T, D], BF16, name="xpp")
             xpps[G] = pl
             for t in range(T):
-                V.tensor_scalar(out=pl[:, t, :], in0=xs[G][:, t, :], scalar1=g32[:, 0, G * T + t : G * T + t + 1], scalar2=None, op0=ALU.mult)
+                V.tensor_scalar(out=pl[:, t, :], in0=xs[G][:, t, :], scalar1=p32[:, G * T + t : G * T + t + 1], scalar2=None, op0=ALU.mult)
 
         def x2(G):
             pl = work.tile([P, T, D], BF16, name="x2p")
@@ -207,19 +222,11 @@ def tile_diagonalfishernaturalgradient_t_kernel(tc, x, a, g_bytes, g_scale, w2, 
             for t in range(T):
                 A.activation(out=pl[:, t, :], in_=xs[G][:, t, :], func=ACT.Square, scale=root[:, 0, G * T + t : G * T + t + 1])
 
-        def i_x(G, which, part, eng):
-            if which == 0 and part == 0:
+        def i_x(G, which, eng, c0, c1):
+            if G not in xis:
                 x_i = work.tile([P, 2, D, T], BF16, name="x_i", align_bytes=64)
                 xis[G] = x_i
-            c = slice(part * D // 2, (part + 1) * D // 2)
-            src = (xpps, x2ps)[which][G][:, :, c].rearrange("p t d -> p d t")
-            dst = xis[G][:, which, c, :]
-            if eng == "P":
-                PO.tensor_scalar(out=dst, in0=src, scalar1=1.0, scalar2=0.0, op0=ALU.mult, op1=ALU.add)
-            elif eng == "V":
-                V.tensor_copy(out=dst, in_=src)
-            else:
-                A.copy(out=dst, in_=src)
+            interleave(xis[G][:, which, c0:c1, :], (xpps, x2ps)[which][G][:, :, c0:c1], eng)
 
         def q_x(G):
             codes = work.tile([P, 2 * D], U32, name="xcodes", align_bytes=64, bufs=3)
@@ -227,21 +234,44 @@ def tile_diagonalfishernaturalgradient_t_kernel(tc, x, a, g_bytes, g_scale, w2, 
             V.quantize_mx(out=codes[:].bitcast(FP8X4), scales=planes[:], in_=xis[G][:].rearrange("p w d t -> p (w d t)"))
             xcs[G] = (codes, planes)
 
-        def s2(G, h0, h1):
-            dc, dp = dcs[G]
+        def s2(G, blk):
+            dc, dp = dcs[G, blk]
             xc, xpl = xcs[G]
-            for acc, w in ((fish, 1), (grad, 0)):
-                for hh in range(h0, h1):
-                    c0 = (2 * hh + w) * HT
+            w = blk[1] - blk[0]
+            for acc, k in ((fish, 1), (grad, 0)):
+                for hh in range(blk[0] // P, blk[1] // P):
+                    c0 = k * w + hh * P - blk[0]
                     PE.matmul_mx(
                         out=acc[hh][:],
                         lhsT=dc[:, c0 : c0 + P].bitcast(FP8X4),
                         lhsT_scale=dp[:, c0 : c0 + P],
-                        rhs=xc[:, w * D : (w + 1) * D].bitcast(FP8X4),
-                        rhs_scale=xpl[:, w * D : (w + 1) * D],
+                        rhs=xc[:, k * D : (k + 1) * D].bitcast(FP8X4),
+                        rhs_scale=xpl[:, k * D : (k + 1) * D],
                         start=(G == 0),
                         stop=(G == GROUPS - 1),
                     )
+
+        NS = GROUPS * T
+        p32 = keep.tile([P, NS], F32, name="p32")
+        negq = keep.tile([P, NS], F32, name="negq")
+        prod = keep.tile([P, 2, NS], F32, name="prod")
+        mag = keep.tile([P, 2, NS], F32, name="mag")
+        r0 = keep.tile([P, 2, NS], F32, name="r0")
+        w0 = keep.tile([P, 2, NS], F32, name="w0")
+        w1 = keep.tile([P, 2, NS], F32, name="w1")
+        z0 = keep.tile([P, 2, NS], F32, name="z0")
+        k0 = keep.tile([P, 2, NS], F32, name="k0")
+        root = keep.tile([P, 2, NS], F32, name="root")
+        w2T = keep.tile([P, KP, H * T], BF16, name="w2T", align_bytes=64)
+        w2c = keep.tile([P, KP, H], U32, name="w2c", align_bytes=64)
+        w2p = keep.tile([P, KP, H], U8, name="w2p", align_bytes=64)
+        w2words = w2s[:].rearrange("p i o -> p (i o)").bitcast(F32)
+        wt = [None, None]
+
+        def w2_copy(g2):
+            V.tensor_copy(
+                out=w2T[:, g2, :].bitcast(F32).rearrange("p (r u) -> p r u", u=2), in_=wt[g2][:].rearrange("p u r -> p r u")
+            )
 
         cast(0, 0, "V")
         cast(0, 1, "A")
@@ -249,151 +279,162 @@ def tile_diagonalfishernaturalgradient_t_kernel(tc, x, a, g_bytes, g_scale, w2, 
         cast(0, 2, "V")
         cast(0, 3, "A")
         tr(0, 1)
-        NS = GROUPS * T
-        g32 = keep.tile([P, 3, NS], F32, name="g32")
-        negq = keep.tile([P, NS], F32, name="negq")
-        prod = keep.tile([P, 2, NS], F32, name="prod")
-        mag = keep.tile([P, 2, NS], F32, name="mag")
-        r0 = keep.tile([P, 2, NS], F32, name="r0")
-        w0 = keep.tile([P, 2, NS], F32, name="w0")
-        z0 = keep.tile([P, 2, NS], F32, name="z0")
-        k0 = keep.tile([P, 2, NS], F32, name="k0")
-        root = keep.tile([P, 2, NS], F32, name="root")
-        V.tensor_copy(out=g32[:], in_=gain[:])
+        ep(0, 0)
+        wt[0] = words_to_bank(w2words, [512 * r for r in range(2)])
+        ep(0, 1)
+        V.tensor_copy(out=p32[:], in_=gain[:, 0, :])
+        V.tensor_tensor(out=prod[:, 0, :], in0=gain[:, 0, :], in1=gain[:, 1, :], op=ALU.mult)
+        V.tensor_tensor(out=prod[:, 1, :], in0=gain[:, 2, :], in1=gain[:, 1, :], op=ALU.mult)
         V.tensor_scalar(out=negq[:], in0=gain[:, 2, :], scalar1=-1.0, scalar2=None, op0=ALU.mult)
-        V.tensor_tensor(out=prod[:, 0, :], in0=g32[:, 0, :], in1=g32[:, 1, :], op=ALU.mult)
-        V.tensor_tensor(out=prod[:, 1, :], in0=g32[:, 2, :], in1=g32[:, 1, :], op=ALU.mult)
         V.scalar_tensor_tensor(out=mag[:], in0=prod[:], scalar=-1.0, in1=prod[:], op0=ALU.mult, op1=ALU.max)
+        xp(0)
+        i_x(0, 0, "P", 0, 256)
+        i_x(0, 0, "P", 256, 512)
         V.tensor_scalar(out=w0[:], in0=mag[:], scalar1=1e-30, scalar2=None, op0=ALU.max)
         A.activation(out=r0[:], in_=w0[:], func=ACT.Abs_reciprocal_sqrt)
-        xp(0)
-        for part in range(2):
-            i_x(0, 0, part, "P")
-        ep(0, 0)
-        w1 = keep.tile([P, 2, NS], F32, name="w1")
-        V.tensor_tensor(out=w1[:], in0=mag[:], in1=r0[:], op=ALU.mult)
-        tr(0, 2)
-        ep(0, 1)
-        V.tensor_tensor(out=z0[:], in0=w1[:], in1=r0[:], op=ALU.mult)
-        tr(0, 3)
-        ep(0, 2)
-        V.tensor_scalar(out=k0[:], in0=z0[:], scalar1=-0.5, scalar2=1.5, op0=ALU.mult, op1=ALU.add)
-        q_g(0, 0)
-        V.tensor_tensor(out=root[:], in0=w1[:], in1=k0[:], op=ALU.mult)
-        w2T = keep.tile([P, KP, H * T], BF16, name="w2T", align_bytes=64)
-        w2c = keep.tile([P, KP, H], U32, name="w2c", align_bytes=64)
-        w2p = keep.tile([P, KP, H], U8, name="w2p", align_bytes=64)
-        w2words = w2s[:].rearrange("p i o -> p (i o)").bitcast(F32)
-        wt = [None, None]
-        wt[0] = words_to_bank(w2words, [512 * r for r in range(2)])
-        ep(0, 3)
         wt[1] = words_to_bank(w2words, [512 * r + 256 for r in range(2)])
-        for t in range(T):
-            cast(1, t, "A")
-        for g2 in range(KP):
-            V.tensor_copy(
-                out=w2T[:, g2, :].bitcast(F32).rearrange("p (r u) -> p r u", u=2), in_=wt[g2][:].rearrange("p u r -> p r u")
-            )
-        q_g(0, 1)
+        w2_copy(0)
+        tr(0, 2)
+        w2_copy(1)
+        tr(0, 3)
+        V.tensor_tensor(out=w1[:], in0=mag[:], in1=r0[:], op=ALU.mult)
+        ep(0, 2)
+        V.tensor_tensor(out=z0[:], in0=w1[:], in1=r0[:], op=ALU.mult)
+        ep(0, 3)
+        V.tensor_scalar(out=k0[:], in0=z0[:], scalar1=-0.5, scalar2=1.5, op0=ALU.mult, op1=ALU.add)
         V.quantize_mx(
             out=w2c[:].rearrange("p g h -> p (g h)").bitcast(FP8X4),
             scales=w2p[:].rearrange("p g h -> p (g h)"),
             in_=w2T[:].rearrange("p g c -> p (g c)"),
         )
-        x2(0)
+        V.tensor_tensor(out=root[:], in0=w1[:], in1=k0[:], op=ALU.mult)
+        cast(1, 0, "A")
+        cast(1, 1, "A")
+        q_g(0, 0)
+        q_g(0, 1)
         tanh2(0)
+        cast(1, 2, "A")
+        cast(1, 3, "A")
+        s1(0)
         tr(1, 0)
         tr(1, 1)
-        s1(0)
-        xp(1)
-        for part in range(2):
-            i_x(0, 1, part, "P")
+        x2(0)
         x2(1)
-        for t in range(T):
-            cast(2, t, "A")
+        cast(2, 0, "A")
+        cast(2, 1, "A")
 
+        W = (0, H)
         for G in range(1, GROUPS):
             L = G - 1
-            for part in range(2):
-                i_x(G, 0, part, "P")
+            if G + 3 < GROUPS:
+                load(G + 3)
+            xp(G)
+            i_x(G, 0, "P", 0, 256)
+            i_x(G, 0, "P", 256, 512)
+            nd(L, W)
+            d2p(L, W)
             ep(G, 0)
             tr(G, 2)
+            i_x(G, 1, "P", 0, 256)
+            i_x(G, 1, "P", 256, 512)
             ep(G, 1)
             tr(G, 3)
-            nd(L, 0)
-            nd(L, 1)
-            d2p(L, 0, 2)
+            if G + 1 < GROUPS:
+                cast(G + 1, 2, "A")
+                cast(G + 1, 3, "A")
             ep(G, 2)
-            for part in range(2):
-                i_x(G, 1, part, "P")
+            if G + 1 < GROUPS:
+                tr(G + 1, 0)
+            d_tile(L, W)
+            for eng, h0, h1 in OPT["id2"]:
+                i_d2(L, W, eng, h0, h1)
             tanh2(G)
             ep(G, 3)
             if G + 1 < GROUPS:
-                tr(G + 1, 0)
                 tr(G + 1, 1)
-            dq(L, 0, 2)
-            i_d2(L, 0, 2, ID2)
+            dq(L, W)
             q_g(G, 0)
-            if L == 0:
-                q_x(0)
             q_g(G, 1)
+            if G == 1:
+                i_x(0, 1, "V", 0, 512)
+                q_x(0)
             s1(G)
-            if G + 2 < GROUPS:
-                for t in range(T):
-                    cast(G + 2, t, "A")
-            if G + 3 < GROUPS:
-                load(G + 3)
-            if G + 1 < GROUPS:
-                xp(G + 1)
-                x2(G + 1)
-            q_d(L, 0, 2)
             q_x(G)
-            s2(L, 0, 2)
+            q_d(L, W)
+            s2(L, W)
+            if G + 1 < GROUPS:
+                x2(G + 1)
+            if G + 2 < GROUPS:
+                cast(G + 2, 0, "A")
+                cast(G + 2, 1, "A")
 
-        ot = keep.tile([P, 4, H], F32, name="ot")
+
         ov = out.rearrange("(t p) h -> p t h", p=P)
         L = GROUPS - 1
-        rr, o1, o2 = {}, {}, {}
+        rr, o1 = {}, {}
         warm3 = keep.tile([P, 1], F32, name="warm3")
 
-        def tail_d(hh):
-            nd(L, hh)
-            d2p(L, hh, hh + 1)
-            dq(L, hh, hh + 1)
-
-        def ratio(hh, c0, c1):
-            n = c1 - c0
-            r_t = work.tile([P, n], F32, name="rr")
-            o1_t = work.tile([P, n], F32, name="o1")
-            o2_t = work.tile([P, n], F32, name="o2")
+        def rsq(hh, c0, c1):
+            r_t = work.tile([P, c1 - c0], F32, name="rr%d" % (c1 - c0), bufs=2)
+            rr[hh, c0] = r_t
             A.activation(out=r_t[:], in_=fish[hh][:, c0:c1], func=ACT.Abs_reciprocal_sqrt, scale=1.0 / N, bias=0.2)
-            V.scalar_tensor_tensor(out=o1_t[:], in0=grad[hh][:, c0:c1], scalar=1.0 / 64.0, in1=r_t[:], op0=ALU.mult, op1=ALU.mult)
-            V.tensor_tensor(out=o2_t[:], in0=o1_t[:], in1=r_t[:], op=ALU.mult)
-            return o2_t
 
-        def turn(hh, c0, c1, o2_t):
+        def square(hh, c0, c1):
+            r_t = work.tile([P, c1 - c0], F32, name="r2", bufs=1)
+            A.activation(out=r_t[:], in_=rr[hh, c0][:], func=ACT.Square)
+            rr[hh, c0] = r_t
+
+        def mul1(hh, c0, c1):
+            o_t = work.tile([P, c1 - c0], F32, name="o1%d" % (c1 - c0), bufs=2)
+            o1[hh, c0] = o_t
+            V.scalar_tensor_tensor(
+                out=o_t[:], in0=grad[hh][:, c0:c1], scalar=1.0 / 64.0, in1=rr[hh, c0][:], op0=ALU.mult, op1=ALU.mult
+            )
+
+        def mul2(hh, c0, c1):
+            o_t = work.tile([P, c1 - c0], F32, name="o2", bufs=2)
+            V.tensor_tensor(out=o_t[:], in0=o1[hh, c0][:], in1=rr[hh, c0][:], op=ALU.mult)
+            o1[hh, c0] = o_t
+
+        def turn(hh, c0, c1, eng):
             m = (c1 - c0) // P
             xt = psum.tile([P, m, P], F32, name="xt", bufs=2)
             for d in range(m):
-                PE.transpose(xt[:, d, :], o2_t[:, d * P : (d + 1) * P], ident[:])
-            dst = ot[:, c0 // P : c1 // P, hh * P : (hh + 1) * P]
-            A.copy(out=dst, in_=xt[:])
-            nc.sync.dma_start(out=ov[:, c0 // P : c1 // P, hh * P : (hh + 1) * P], in_=dst)
+                PE.transpose(xt[:, d, :], o1[hh, c0][:, d * P : (d + 1) * P], ident[:])
+            ot = work.tile([P, m, P], F32, name="ot%d" % m, bufs=2)
+            if eng == "A":
+                A.copy(out=ot[:], in_=xt[:])
+            else:
+                V.tensor_copy(out=ot[:], in_=xt[:])
+            nc.sync.dma_start(out=ov[:, c0 // P : c1 // P, hh * P : (hh + 1) * P], in_=ot[:])
 
-        tail_d(0)
-        tail_d(1)
-        i_d2(L, 0, 1, "V")
-        i_d2(L, 1, 2, "V")
-        q_d(L, 0, 1)
-        s2(L, 0, 1)
-        q_d(L, 1, 2)
-        s2(L, 1, 2)
+        B0, B1 = blocks(L)
+        nd(L, B0)
+        d2p(L, B0)
+        nd(L, B1)
+        d2p(L, B1)
         A.activation(out=warm3[:], in_=warm[:], func=ACT.Abs_reciprocal_sqrt)
-        parts = [(hh, c0) for hh in range(2) for c0 in (0, 256)]
-        pend = None
-        for hh, c0 in parts:
-            o = ratio(hh, c0, c0 + 256)
-            if pend is not None:
-                turn(*pend)
-            pend = (hh, c0, c0 + 256, o)
-        turn(*pend)
+        d_tile(L, B0)
+        dq(L, B0)
+        i_d2(L, B0, "V", 0, HT)
+        d_tile(L, B1)
+        dq(L, B1)
+        q_d(L, B0)
+        s2(L, B0)
+        i_d2(L, B1, "V", 0, HT)
+        q_d(L, B1)
+        s2(L, B1)
+        a0, b0, a1, b1 = [(hh, c, c + 256) for hh in range(2) for c in (0, 256)]
+        all0 = (0, 0, 512)
+        rsq(*all0)
+        square(*all0)
+        mul1(*all0)
+        rsq(*a1)
+        rsq(*b1)
+        mul1(*a1)
+        mul1(*b1)
+        turn(*all0, "A")
+        mul2(*a1)
+        mul2(*b1)
+        turn(*a1, "A")
+        turn(*b1, "V")

@@ -23,7 +23,6 @@ KP = O // GROUP
 
 
 HT = H // 2
-OPT = {"id2": [("P", 0, 128), ("A", 128, 256)]}
 
 
 def tile_diagonalfishernaturalgradient_t_kernel(tc, x, a, g_bytes, g_scale, w2, p, q, s, out):
@@ -56,15 +55,18 @@ def tile_diagonalfishernaturalgradient_t_kernel(tc, x, a, g_bytes, g_scale, w2, 
             g_t = loads.tile([P, T * O], U8, name="g_t")
             x_t = loads.tile([P, T, D], BF16, name="x_t")
             a_t = loads.tile([P, T * H], BF16, name="a_t")
+            gb[G], xs[G], as_[G] = g_t, x_t, a_t
             if G == 0:
                 nc.sync.dma_start(out=g_t[:, : 2 * O], in_=gv[G][:, : 2 * O])
                 nc.sync.dma_start(out=g_t[:, 2 * O :], in_=gv[G][:, 2 * O :])
+                nc.sync.dma_start(out=x_t[:].rearrange("p t d -> p (t d)"), in_=xv[G])
+                return
+            nc.sync.dma_start(out=g_t[:], in_=gv[G])
+            if G == 1:
                 nc.sync.dma_start(out=w2s[:], in_=w2.rearrange("(i r) o -> r i o", r=P))
-            else:
-                nc.sync.dma_start(out=g_t[:], in_=gv[G])
+                nc.sync.dma_start(out=as_[0][:], in_=av[0])
             nc.sync.dma_start(out=x_t[:].rearrange("p t d -> p (t d)"), in_=xv[G])
             nc.sync.dma_start(out=a_t[:], in_=av[G])
-            gb[G], xs[G], as_[G] = g_t, x_t, a_t
 
         ident = keep.tile([P, P], F32, name="ident")
         make_identity(nc, ident[:])
@@ -86,7 +88,7 @@ def tile_diagonalfishernaturalgradient_t_kernel(tc, x, a, g_bytes, g_scale, w2, 
             d4 = dst.rearrange("p (c i) t -> p c t i", i=4)
             s4 = src.rearrange("p t (c i) -> p c t i", i=4)
             if eng == "P":
-                PO.tensor_scalar(out=d4, in0=s4, scalar1=1.0, scalar2=0.0, op0=ALU.mult, op1=ALU.add)
+                PO.tensor_scalar(out=dst, in0=src.rearrange("p t c -> p c t"), scalar1=1.0, scalar2=0.0, op0=ALU.mult, op1=ALU.add)
             elif eng == "V":
                 V.tensor_copy(out=d4, in_=s4)
             else:
@@ -162,7 +164,9 @@ def tile_diagonalfishernaturalgradient_t_kernel(tc, x, a, g_bytes, g_scale, w2, 
             th = work.tile([P, T * H], F32, name="th")
             sq = work.tile([P, T, H], F32, name="sq")
             A.activation(out=th[:], in_=as_[G][:], func=ACT.Tanh)
-            A.activation(out=sq[:].rearrange("p t h -> p (t h)"), in_=th[:], func=ACT.Square)
+            for t in range(T):
+                j = G * T + t
+                A.activation(out=sq[:, t, :], in_=th[:, t * H : (t + 1) * H], func=ACT.Square, scale=root[:, 1, j : j + 1])
             sqd[G] = sq
 
         def nd(G, blk):
@@ -170,35 +174,36 @@ def tile_diagonalfishernaturalgradient_t_kernel(tc, x, a, g_bytes, g_scale, w2, 
             n_t = work.tile([P, T, w], F32, name="nd%d" % w)
             nds[G, blk] = n_t
             for t0, nt, b in bk[G, blk]:
-                V.scalar_tensor_tensor(
-                    out=n_t[:, t0 : t0 + nt, :],
-                    in0=sqd[G][:, t0 : t0 + nt, blk[0] : blk[1]],
-                    scalar=1.0,
-                    in1=b[:],
-                    op0=ALU.subtract,
-                    op1=ALU.mult,
-                )
+                for i in range(nt):
+                    j = G * T + t0 + i
+                    V.scalar_tensor_tensor(
+                        out=n_t[:, t0 + i, :],
+                        in0=sqd[G][:, t0 + i, blk[0] : blk[1]],
+                        scalar=q32[:, j : j + 1],
+                        in1=b[:, i, :],
+                        op0=ALU.subtract,
+                        op1=ALU.mult,
+                    )
 
         def d_tile(G, blk):
             w = blk[1] - blk[0]
             d_i = work.tile([P, 2, w, T], BF16, name="d_i%d" % w, align_bytes=64)
             dis[G, blk] = d_i
 
-        def dq(G, blk):
-            w = blk[1] - blk[0]
-            V.tensor_tensor(
-                out=dis[G, blk][:, 0],
-                in0=nds[G, blk][:].rearrange("p t h -> p h t"),
-                in1=negq[:, G * T : (G + 1) * T].rearrange("p (b t) -> p b t", b=1).to_broadcast([P, w, T]),
-                op=ALU.mult,
-            )
+        def dq(G, blk, eng, h0, h1):
+            d4 = dis[G, blk][:, 0, h0:h1, :].rearrange("p (c i) t -> p c t i", i=4)
+            s4 = nds[G, blk][:, :, h0:h1].rearrange("p t (c i) -> p c t i", i=4)
+            if eng == "V":
+                V.tensor_scalar(out=d4, in0=s4, scalar1=-1.0, scalar2=None, op0=ALU.mult)
+            else:
+                A.activation(out=d4, in_=s4, func=ACT.Copy, scale=-1.0)
 
         def d2p(G, blk):
             w = blk[1] - blk[0]
             pl = work.tile([P, T, w], BF16, name="d2p%d" % w)
             d2ps[G, blk] = pl
             for t in range(T):
-                A.activation(out=pl[:, t, :], in_=nds[G, blk][:, t, :], func=ACT.Square, scale=root[:, 1, G * T + t : G * T + t + 1])
+                A.activation(out=pl[:, t, :], in_=nds[G, blk][:, t, :], func=ACT.Square, scale=c2[:, G * T + t : G * T + t + 1])
 
         def i_d2(G, blk, eng, h0, h1):
             interleave(dis[G, blk][:, 1, h0:h1, :], d2ps[G, blk][:, :, h0:h1], eng)
@@ -210,10 +215,12 @@ def tile_diagonalfishernaturalgradient_t_kernel(tc, x, a, g_bytes, g_scale, w2, 
             dcs[G, blk] = (codes, planes)
             V.quantize_mx(out=codes[:].bitcast(FP8X4), scales=planes[:], in_=dis[G, blk][:].rearrange("p w h t -> p (w h t)"))
 
-        def xp(G):
-            pl = work.tile([P, T, D], BF16, name="xpp")
-            xpps[G] = pl
-            for t in range(T):
+        def xp(G, slots=range(T)):
+            if G not in xpps:
+                pl = work.tile([P, T, D], BF16, name="xpp")
+                xpps[G] = pl
+            pl = xpps[G]
+            for t in slots:
                 V.tensor_scalar(out=pl[:, t, :], in0=xs[G][:, t, :], scalar1=p32[:, G * T + t : G * T + t + 1], scalar2=None, op0=ALU.mult)
 
         def x2(G):
@@ -253,15 +260,17 @@ def tile_diagonalfishernaturalgradient_t_kernel(tc, x, a, g_bytes, g_scale, w2, 
 
         NS = GROUPS * T
         p32 = keep.tile([P, NS], F32, name="p32")
-        negq = keep.tile([P, NS], F32, name="negq")
-        prod = keep.tile([P, 2, NS], F32, name="prod")
-        mag = keep.tile([P, 2, NS], F32, name="mag")
-        r0 = keep.tile([P, 2, NS], F32, name="r0")
-        w0 = keep.tile([P, 2, NS], F32, name="w0")
-        w1 = keep.tile([P, 2, NS], F32, name="w1")
-        z0 = keep.tile([P, 2, NS], F32, name="z0")
-        k0 = keep.tile([P, 2, NS], F32, name="k0")
-        root = keep.tile([P, 2, NS], F32, name="root")
+        prod = keep.tile([P, 3, NS], F32, name="prod")
+        mag = keep.tile([P, 3, NS], F32, name="mag")
+        r0 = keep.tile([P, 3, NS], F32, name="r0")
+        w0 = keep.tile([P, 3, NS], F32, name="w0")
+        w1 = keep.tile([P, 3, NS], F32, name="w1")
+        z0 = keep.tile([P, 3, NS], F32, name="z0")
+        k0 = keep.tile([P, 3, NS], F32, name="k0")
+        root = keep.tile([P, 3, NS], F32, name="root")
+        q32 = keep.tile([P, NS], F32, name="q32")
+        rq = keep.tile([P, NS], F32, name="rq")
+        c2 = keep.tile([P, NS], F32, name="c2")
         w2T = keep.tile([P, KP, H * T], BF16, name="w2T", align_bytes=64)
         w2c = keep.tile([P, KP, H], U32, name="w2c", align_bytes=64)
         w2p = keep.tile([P, KP, H], U8, name="w2p", align_bytes=64)
@@ -269,7 +278,7 @@ def tile_diagonalfishernaturalgradient_t_kernel(tc, x, a, g_bytes, g_scale, w2, 
         wt = [None, None]
 
         def w2_copy(g2):
-            V.tensor_copy(
+            A.copy(
                 out=w2T[:, g2, :].bitcast(F32).rearrange("p (r u) -> p r u", u=2), in_=wt[g2][:].rearrange("p u r -> p r u")
             )
 
@@ -280,45 +289,53 @@ def tile_diagonalfishernaturalgradient_t_kernel(tc, x, a, g_bytes, g_scale, w2, 
         cast(0, 3, "A")
         tr(0, 1)
         ep(0, 0)
-        wt[0] = words_to_bank(w2words, [512 * r for r in range(2)])
+        tr(0, 2)
         ep(0, 1)
-        V.tensor_copy(out=p32[:], in_=gain[:, 0, :])
+        tr(0, 3)
         V.tensor_tensor(out=prod[:, 0, :], in0=gain[:, 0, :], in1=gain[:, 1, :], op=ALU.mult)
-        V.tensor_tensor(out=prod[:, 1, :], in0=gain[:, 2, :], in1=gain[:, 1, :], op=ALU.mult)
-        V.tensor_scalar(out=negq[:], in0=gain[:, 2, :], scalar1=-1.0, scalar2=None, op0=ALU.mult)
+        V.tensor_tensor(out=prod[:, 2, :], in0=gain[:, 2, :], in1=gain[:, 1, :], op=ALU.mult)
+        V.tensor_copy(out=prod[:, 1, :], in_=gain[:, 2, :])
+        V.tensor_copy(out=p32[:], in_=gain[:, 0, :])
         V.scalar_tensor_tensor(out=mag[:], in0=prod[:], scalar=-1.0, in1=prod[:], op0=ALU.mult, op1=ALU.max)
-        xp(0)
-        i_x(0, 0, "P", 0, 256)
-        i_x(0, 0, "P", 256, 512)
         V.tensor_scalar(out=w0[:], in0=mag[:], scalar1=1e-30, scalar2=None, op0=ALU.max)
         A.activation(out=r0[:], in_=w0[:], func=ACT.Abs_reciprocal_sqrt)
+        xp(0, (0, 1))
+        V.tensor_tensor(out=w1[:], in0=mag[:], in1=r0[:], op=ALU.mult)
+        V.reciprocal(out=rq[:], in_=w0[:, 1, :])
+        V.tensor_tensor(out=z0[:], in0=w1[:], in1=r0[:], op=ALU.mult)
+        xp(0, (2,))
+        V.tensor_scalar(out=k0[:], in0=z0[:], scalar1=-0.5, scalar2=1.5, op0=ALU.mult, op1=ALU.add)
+        V.tensor_tensor(out=root[:], in0=w1[:], in1=k0[:], op=ALU.mult)
+        V.tensor_tensor(out=q32[:], in0=root[:, 1, :], in1=root[:, 1, :], op=ALU.mult)
+        V.tensor_tensor(out=c2[:], in0=root[:, 2, :], in1=rq[:], op=ALU.mult)
+        xp(0, (3,))
+        i_x(0, 0, "P", 0, 192)
+        i_x(0, 0, "P", 192, 384)
+        x2(0)
+        ep(0, 2)
+        wt[0] = words_to_bank(w2words, [512 * r for r in range(2)])
+        ep(0, 3)
         wt[1] = words_to_bank(w2words, [512 * r + 256 for r in range(2)])
         w2_copy(0)
-        tr(0, 2)
         w2_copy(1)
-        tr(0, 3)
-        V.tensor_tensor(out=w1[:], in0=mag[:], in1=r0[:], op=ALU.mult)
-        ep(0, 2)
-        V.tensor_tensor(out=z0[:], in0=w1[:], in1=r0[:], op=ALU.mult)
-        ep(0, 3)
-        V.tensor_scalar(out=k0[:], in0=z0[:], scalar1=-0.5, scalar2=1.5, op0=ALU.mult, op1=ALU.add)
+        cast(1, 1, "A")
+        cast(1, 3, "A")
+        i_x(0, 0, "V", 384, 512)
+        q_g(0, 0)
+        q_g(0, 1)
+        cast(1, 0, "V")
         V.quantize_mx(
             out=w2c[:].rearrange("p g h -> p (g h)").bitcast(FP8X4),
             scales=w2p[:].rearrange("p g h -> p (g h)"),
             in_=w2T[:].rearrange("p g c -> p (g c)"),
         )
-        V.tensor_tensor(out=root[:], in0=w1[:], in1=k0[:], op=ALU.mult)
-        cast(1, 0, "A")
-        cast(1, 1, "A")
-        q_g(0, 0)
-        q_g(0, 1)
+        cast(1, 2, "V")
         tanh2(0)
-        cast(1, 2, "A")
-        cast(1, 3, "A")
         s1(0)
         tr(1, 0)
         tr(1, 1)
-        x2(0)
+        i_x(0, 1, "V", 0, 512)
+        q_x(0)
         x2(1)
         cast(2, 0, "A")
         cast(2, 1, "A")
@@ -335,30 +352,27 @@ def tile_diagonalfishernaturalgradient_t_kernel(tc, x, a, g_bytes, g_scale, w2, 
             d2p(L, W)
             ep(G, 0)
             tr(G, 2)
-            i_x(G, 1, "P", 0, 256)
-            i_x(G, 1, "P", 256, 512)
+            i_x(G, 1, "P", 0, 224)
+            i_x(G, 1, "P", 224, 448)
             ep(G, 1)
             tr(G, 3)
+            d_tile(L, W)
+            dq(L, W, "A", 0, 256)
             if G + 1 < GROUPS:
                 cast(G + 1, 2, "A")
                 cast(G + 1, 3, "A")
             ep(G, 2)
             if G + 1 < GROUPS:
                 tr(G + 1, 0)
-            d_tile(L, W)
-            for eng, h0, h1 in OPT["id2"]:
-                i_d2(L, W, eng, h0, h1)
             tanh2(G)
             ep(G, 3)
             if G + 1 < GROUPS:
                 tr(G + 1, 1)
-            dq(L, W)
             q_g(G, 0)
             q_g(G, 1)
-            if G == 1:
-                i_x(0, 1, "V", 0, 512)
-                q_x(0)
             s1(G)
+            i_x(G, 1, "V", 448, 512)
+            i_d2(L, W, "V", 0, H)
             q_x(G)
             q_d(L, W)
             s2(L, W)
@@ -415,25 +429,25 @@ def tile_diagonalfishernaturalgradient_t_kernel(tc, x, a, g_bytes, g_scale, w2, 
         d2p(L, B1)
         A.activation(out=warm3[:], in_=warm[:], func=ACT.Abs_reciprocal_sqrt)
         d_tile(L, B0)
-        dq(L, B0)
+        dq(L, B0, "V", 0, HT)
         i_d2(L, B0, "V", 0, HT)
         d_tile(L, B1)
-        dq(L, B1)
+        i_d2(L, B1, "V", 0, HT)
         q_d(L, B0)
         s2(L, B0)
-        i_d2(L, B1, "V", 0, HT)
-        q_d(L, B1)
-        s2(L, B1)
+        dq(L, B1, "V", 0, HT)
         a0, b0, a1, b1 = [(hh, c, c + 256) for hh in range(2) for c in (0, 256)]
         all0 = (0, 0, 512)
         rsq(*all0)
         square(*all0)
+        q_d(L, B1)
+        s2(L, B1)
         mul1(*all0)
         rsq(*a1)
         rsq(*b1)
+        turn(*all0, "A")
         mul1(*a1)
         mul1(*b1)
-        turn(*all0, "A")
         mul2(*a1)
         mul2(*b1)
         turn(*a1, "A")

from contextlib import ExitStack

import concourse.mybir as mybir
from concourse.masks import make_identity

N, D, H, O = 4096, 512, 256, 1024
FLOPS = 2 * N * O * H + 2 * (2 * N * D * H)

F32 = mybir.dt.float32
BF16 = mybir.dt.bfloat16
U32 = mybir.dt.uint32
U8 = mybir.dt.uint8
FP8 = mybir.dt.float8_e4m3fn
FP8X4 = mybir.dt.float8_e4m3fn_x4
ACT = mybir.ActivationFunctionType
ALU = mybir.AluOpType

P = 128
T = 4
GROUP = P * T
GROUPS = N // GROUP
KP = O // GROUP


HT = H // 2


def tile_diagonalfishernaturalgradient_t_kernel(tc, x, a, g_bytes, g_scale, w2, p, q, s, out):
    nc = tc.nc
    with ExitStack() as ctx:
        keep = ctx.enter_context(tc.tile_pool(name="keep", bufs=1))
        loads = ctx.enter_context(tc.tile_pool(name="loads", bufs=4))
        work = ctx.enter_context(tc.tile_pool(name="work", bufs=2))
        psum = ctx.enter_context(tc.psum_pool(name="psum", bufs=1))
        ctx.enter_context(tc.manual_schedule())

        V, A, PO, PE = nc.vector, nc.scalar, nc.gpsimd, nc.tensor

        warm = keep.tile([P, 1], F32, name="warm")
        V.memset(warm[:], 1.0)
        warm2 = keep.tile([P, 1], F32, name="warm2")
        A.activation(out=warm2[:], in_=warm[:], func=ACT.Abs_reciprocal_sqrt)
        gain = keep.tile([P, 3, GROUPS * T], BF16, name="gain")
        scale4 = keep.tile([P, KP, T], F32, name="scale4")
        A.dma_start(out=scale4[:], in_=g_scale.rearrange("o (g p t) -> p (o g) t", p=P, t=T))
        for i, v in enumerate((p, s, q)):
            A.dma_start(out=gain[:, i, :].rearrange("p (g t) -> p g t", t=T), in_=v.rearrange("(g p t) -> p g t", p=P, t=T))
        gb, xs, as_ = {}, {}, {}
        xv = x.rearrange("(g p t) d -> g p (t d)", p=P, t=T)
        av = a.rearrange("(g p t) h -> g p (t h)", p=P, t=T)
        gv = g_bytes.rearrange("(g p t) o -> g p (t o)", p=P, t=T)
        w2s = keep.tile([P, 2, O], BF16, name="w2s")

        def load(G):
            g_t = loads.tile([P, T * O], U8, name="g_t")
            x_t = loads.tile([P, T, D], BF16, name="x_t")
            a_t = loads.tile([P, T * H], BF16, name="a_t")
            gb[G], xs[G], as_[G] = g_t, x_t, a_t
            if G == 0:
                nc.sync.dma_start(out=g_t[:, : 2 * O], in_=gv[G][:, : 2 * O])
                nc.sync.dma_start(out=g_t[:, 2 * O :], in_=gv[G][:, 2 * O :])
                nc.sync.dma_start(out=x_t[:].rearrange("p t d -> p (t d)"), in_=xv[G])
                return
            nc.sync.dma_start(out=g_t[:], in_=gv[G])
            if G == 1:
                nc.sync.dma_start(out=w2s[:], in_=w2.rearrange("(i r) o -> r i o", r=P))
                nc.sync.dma_start(out=as_[0][:], in_=av[0])
            nc.sync.dma_start(out=x_t[:].rearrange("p t d -> p (t d)"), in_=xv[G])
            nc.sync.dma_start(out=a_t[:], in_=av[G])

        ident = keep.tile([P, P], F32, name="ident")
        make_identity(nc, ident[:])
        for G in range(4):
            load(G)

        gc, gT, gq, bk, sqd, nds, d2ps, dis, dcs, xpps, x2ps, xis, xcs, trs = ({} for _ in range(14))
        grad, fish = [], []
        for hh in range(2):
            g_acc = psum.tile([P, D], F32, name="grad%d" % hh)
            f_acc = psum.tile([P, D], F32, name="fish%d" % hh)
            grad.append(g_acc)
            fish.append(f_acc)

        def blocks(G):
            return [(0, H)] if G < GROUPS - 1 else [(0, HT), (HT, H)]

        def interleave(dst, src, eng):
            d4 = dst.rearrange("p (c i) t -> p c t i", i=4)
            s4 = src.rearrange("p t (c i) -> p c t i", i=4)
            if eng == "P":
                PO.tensor_scalar(out=dst, in0=src.rearrange("p t c -> p c t"), scalar1=1.0, scalar2=0.0, op0=ALU.mult, op1=ALU.add)
            elif eng == "V":
                V.tensor_copy(out=d4, in_=s4)
            else:
                A.copy(out=d4, in_=s4)

        def cast(G, t, eng):
            if G not in gc:
                c = work.tile([P, T, O], BF16, name="gc", bufs=3)
                gc[G] = c
            src = gb[G][:, t * O : (t + 1) * O].bitcast(FP8)
            if eng == "V":
                V.tensor_copy(out=gc[G][:, t, :], in_=src)
            else:
                A.copy(out=gc[G][:, t, :], in_=src)

        def words_to_bank(words, starts):
            xt = psum.tile([P, 2, 2 * P], F32, name="xt", bufs=2)
            for i in range(2):
                for u in range(2):
                    PE.transpose(xt[:, u, i * P : (i + 1) * P], words[:, starts[i] + u : starts[i] + 256 : 2], ident[:])
            return xt

        def tr(G, b):
            g2, tp = b // 2, b % 2
            words = gc[G][:].rearrange("p t k -> p (t k)").bitcast(F32)
            trs[G, b] = words_to_bank(words, [512 * (2 * tp + i) + 256 * g2 for i in range(2)])

        def ep(G, b):
            g2, tp = b // 2, b % 2
            if b == 0:
                gT_t = work.tile([P, KP, T * P * T], BF16, name="gT", align_bytes=64)
                gT[G] = gT_t
            V.tensor_tensor(
                out=gT[G][:, g2, tp * 1024 : (tp + 1) * 1024].rearrange("p (r u e) -> p r u e", u=2, e=2),
                in0=trs[G, b][:].bitcast(BF16).rearrange("p u (r e) -> p r u e", e=2),
                in1=scale4[:, g2 : g2 + 1, :].to_broadcast([P, 256, T]).rearrange("p r (u e) -> p r u e", e=2),
                op=ALU.mult,
            )

        def q_g(G, g2):
            if g2 == 0:
                codes = work.tile([P, KP, T * P], U32, name="gcodes", align_bytes=64)
                planes = work.tile([P, KP, T * P], U8, name="gplanes", align_bytes=64)
                gq[G] = (codes, planes)
            codes, planes = gq[G]
            V.quantize_mx(out=codes[:, g2, :].bitcast(FP8X4), scales=planes[:, g2, :], in_=gT[G][:, g2, :])

        def s1(G):
            codes, planes = gq[G]
            n = 0
            for blk in blocks(G):
                w = blk[1] - blk[0]
                nt = 512 // w
                bk[G, blk] = []
                for t0 in range(0, T, nt):
                    b = psum.tile([P, nt, w], F32, name="bk%d" % n)
                    n += 1
                    bk[G, blk].append((t0, nt, b))
                    for i in range(nt):
                        c = slice((t0 + i) * P, (t0 + i + 1) * P)
                        for g2 in range(KP):
                            PE.matmul_mx(
                                out=b[:, i, :],
                                lhsT=codes[:, g2, c].bitcast(FP8X4),
                                lhsT_scale=planes[:, g2, c],
                                rhs=w2c[:, g2, blk[0] : blk[1]].bitcast(FP8X4),
                                rhs_scale=w2p[:, g2, blk[0] : blk[1]],
                                start=(g2 == 0),
                                stop=(g2 == KP - 1),
                            )

        def tanh2(G):
            th = work.tile([P, T * H], F32, name="th")
            sq = work.tile([P, T, H], F32, name="sq")
            A.activation(out=th[:], in_=as_[G][:], func=ACT.Tanh)
            for t in range(T):
                j = G * T + t
                A.activation(out=sq[:, t, :], in_=th[:, t * H : (t + 1) * H], func=ACT.Square, scale=root[:, 1, j : j + 1])
            sqd[G] = sq

        def nd(G, blk):
            w = blk[1] - blk[0]
            n_t = work.tile([P, T, w], F32, name="nd%d" % w)
            nds[G, blk] = n_t
            for t0, nt, b in bk[G, blk]:
                for i in range(nt):
                    j = G * T + t0 + i
                    V.scalar_tensor_tensor(
                        out=n_t[:, t0 + i, :],
                        in0=sqd[G][:, t0 + i, blk[0] : blk[1]],
                        scalar=q32[:, j : j + 1],
                        in1=b[:, i, :],
                        op0=ALU.subtract,
                        op1=ALU.mult,
                    )

        def d_tile(G, blk):
            w = blk[1] - blk[0]
            d_i = work.tile([P, 2, w, T], BF16, name="d_i%d" % w, align_bytes=64)
            dis[G, blk] = d_i

        def dq(G, blk, eng, h0, h1):
            d4 = dis[G, blk][:, 0, h0:h1, :].rearrange("p (c i) t -> p c t i", i=4)
            s4 = nds[G, blk][:, :, h0:h1].rearrange("p t (c i) -> p c t i", i=4)
            if eng == "V":
                V.tensor_scalar(out=d4, in0=s4, scalar1=-1.0, scalar2=None, op0=ALU.mult)
            else:
                A.activation(out=d4, in_=s4, func=ACT.Copy, scale=-1.0)

        def d2p(G, blk):
            w = blk[1] - blk[0]
            pl = work.tile([P, T, w], BF16, name="d2p%d" % w)
            d2ps[G, blk] = pl
            for t in range(T):
                A.activation(out=pl[:, t, :], in_=nds[G, blk][:, t, :], func=ACT.Square, scale=c2[:, G * T + t : G * T + t + 1])

        def i_d2(G, blk, eng, h0, h1):
            interleave(dis[G, blk][:, 1, h0:h1, :], d2ps[G, blk][:, :, h0:h1], eng)

        def q_d(G, blk):
            w = blk[1] - blk[0]
            codes = work.tile([P, 2 * w], U32, name="dcodes%d" % w, align_bytes=64)
            planes = work.tile([P, 2 * w], U8, name="dplanes%d" % w, align_bytes=64)
            dcs[G, blk] = (codes, planes)
            V.quantize_mx(out=codes[:].bitcast(FP8X4), scales=planes[:], in_=dis[G, blk][:].rearrange("p w h t -> p (w h t)"))

        def xp(G, slots=range(T)):
            if G not in xpps:
                pl = work.tile([P, T, D], BF16, name="xpp")
                xpps[G] = pl
            pl = xpps[G]
            for t in slots:
                V.tensor_scalar(out=pl[:, t, :], in0=xs[G][:, t, :], scalar1=p32[:, G * T + t : G * T + t + 1], scalar2=None, op0=ALU.mult)

        def x2(G):
            pl = work.tile([P, T, D], BF16, name="x2p")
            x2ps[G] = pl
            for t in range(T):
                A.activation(out=pl[:, t, :], in_=xs[G][:, t, :], func=ACT.Square, scale=root[:, 0, G * T + t : G * T + t + 1])

        def i_x(G, which, eng, c0, c1):
            if G not in xis:
                x_i = work.tile([P, 2, D, T], BF16, name="x_i", align_bytes=64)
                xis[G] = x_i
            interleave(xis[G][:, which, c0:c1, :], (xpps, x2ps)[which][G][:, :, c0:c1], eng)

        def q_x(G):
            codes = work.tile([P, 2 * D], U32, name="xcodes", align_bytes=64, bufs=3)
            planes = work.tile([P, 2 * D], U8, name="xplanes", align_bytes=64, bufs=3)
            V.quantize_mx(out=codes[:].bitcast(FP8X4), scales=planes[:], in_=xis[G][:].rearrange("p w d t -> p (w d t)"))
            xcs[G] = (codes, planes)

        def s2(G, blk):
            dc, dp = dcs[G, blk]
            xc, xpl = xcs[G]
            w = blk[1] - blk[0]
            for acc, k in ((fish, 1), (grad, 0)):
                for hh in range(blk[0] // P, blk[1] // P):
                    c0 = k * w + hh * P - blk[0]
                    PE.matmul_mx(
                        out=acc[hh][:],
                        lhsT=dc[:, c0 : c0 + P].bitcast(FP8X4),
                        lhsT_scale=dp[:, c0 : c0 + P],
                        rhs=xc[:, k * D : (k + 1) * D].bitcast(FP8X4),
                        rhs_scale=xpl[:, k * D : (k + 1) * D],
                        start=(G == 0),
                        stop=(G == GROUPS - 1),
                    )

        NS = GROUPS * T
        p32 = keep.tile([P, NS], F32, name="p32")
        prod = keep.tile([P, 3, NS], F32, name="prod")
        mag = keep.tile([P, 3, NS], F32, name="mag")
        r0 = keep.tile([P, 3, NS], F32, name="r0")
        w0 = keep.tile([P, 3, NS], F32, name="w0")
        w1 = keep.tile([P, 3, NS], F32, name="w1")
        z0 = keep.tile([P, 3, NS], F32, name="z0")
        k0 = keep.tile([P, 3, NS], F32, name="k0")
        root = keep.tile([P, 3, NS], F32, name="root")
        q32 = keep.tile([P, NS], F32, name="q32")
        rq = keep.tile([P, NS], F32, name="rq")
        c2 = keep.tile([P, NS], F32, name="c2")
        w2T = keep.tile([P, KP, H * T], BF16, name="w2T", align_bytes=64)
        w2c = keep.tile([P, KP, H], U32, name="w2c", align_bytes=64)
        w2p = keep.tile([P, KP, H], U8, name="w2p", align_bytes=64)
        w2words = w2s[:].rearrange("p i o -> p (i o)").bitcast(F32)
        wt = [None, None]

        def w2_copy(g2):
            A.copy(
                out=w2T[:, g2, :].bitcast(F32).rearrange("p (r u) -> p r u", u=2), in_=wt[g2][:].rearrange("p u r -> p r u")
            )

        cast(0, 0, "V")
        cast(0, 1, "A")
        tr(0, 0)
        cast(0, 2, "V")
        cast(0, 3, "A")
        tr(0, 1)
        ep(0, 0)
        tr(0, 2)
        ep(0, 1)
        tr(0, 3)
        V.tensor_tensor(out=prod[:, 0, :], in0=gain[:, 0, :], in1=gain[:, 1, :], op=ALU.mult)
        V.tensor_tensor(out=prod[:, 2, :], in0=gain[:, 2, :], in1=gain[:, 1, :], op=ALU.mult)
        V.tensor_copy(out=prod[:, 1, :], in_=gain[:, 2, :])
        V.tensor_copy(out=p32[:], in_=gain[:, 0, :])
        V.scalar_tensor_tensor(out=mag[:], in0=prod[:], scalar=-1.0, in1=prod[:], op0=ALU.mult, op1=ALU.max)
        V.tensor_scalar(out=w0[:], in0=mag[:], scalar1=1e-30, scalar2=None, op0=ALU.max)
        A.activation(out=r0[:], in_=w0[:], func=ACT.Abs_reciprocal_sqrt)
        xp(0, (0, 1))
        V.tensor_tensor(out=w1[:], in0=mag[:], in1=r0[:], op=ALU.mult)
        V.reciprocal(out=rq[:], in_=w0[:, 1, :])
        V.tensor_tensor(out=z0[:], in0=w1[:], in1=r0[:], op=ALU.mult)
        xp(0, (2,))
        V.tensor_scalar(out=k0[:], in0=z0[:], scalar1=-0.5, scalar2=1.5, op0=ALU.mult, op1=ALU.add)
        V.tensor_tensor(out=root[:], in0=w1[:], in1=k0[:], op=ALU.mult)
        V.tensor_tensor(out=q32[:], in0=root[:, 1, :], in1=root[:, 1, :], op=ALU.mult)
        V.tensor_tensor(out=c2[:], in0=root[:, 2, :], in1=rq[:], op=ALU.mult)
        xp(0, (3,))
        i_x(0, 0, "P", 0, 192)
        i_x(0, 0, "P", 192, 384)
        x2(0)
        ep(0, 2)
        wt[0] = words_to_bank(w2words, [512 * r for r in range(2)])
        ep(0, 3)
        wt[1] = words_to_bank(w2words, [512 * r + 256 for r in range(2)])
        w2_copy(0)
        w2_copy(1)
        cast(1, 1, "A")
        cast(1, 3, "A")
        i_x(0, 0, "V", 384, 512)
        q_g(0, 0)
        q_g(0, 1)
        cast(1, 0, "V")
        V.quantize_mx(
            out=w2c[:].rearrange("p g h -> p (g h)").bitcast(FP8X4),
            scales=w2p[:].rearrange("p g h -> p (g h)"),
            in_=w2T[:].rearrange("p g c -> p (g c)"),
        )
        cast(1, 2, "V")
        tanh2(0)
        s1(0)
        tr(1, 0)
        tr(1, 1)
        i_x(0, 1, "V", 0, 512)
        q_x(0)
        x2(1)
        cast(2, 0, "A")
        cast(2, 1, "A")

        W = (0, H)
        for G in range(1, GROUPS):
            L = G - 1
            if G + 3 < GROUPS:
                load(G + 3)
            xp(G)
            i_x(G, 0, "P", 0, 256)
            i_x(G, 0, "P", 256, 512)
            nd(L, W)
            d2p(L, W)
            ep(G, 0)
            tr(G, 2)
            i_x(G, 1, "P", 0, 224)
            i_x(G, 1, "P", 224, 448)
            ep(G, 1)
            tr(G, 3)
            d_tile(L, W)
            dq(L, W, "A", 0, 256)
            if G + 1 < GROUPS:
                cast(G + 1, 2, "A")
                cast(G + 1, 3, "A")
            ep(G, 2)
            if G + 1 < GROUPS:
                tr(G + 1, 0)
            tanh2(G)
            ep(G, 3)
            if G + 1 < GROUPS:
                tr(G + 1, 1)
            q_g(G, 0)
            q_g(G, 1)
            s1(G)
            i_x(G, 1, "V", 448, 512)
            i_d2(L, W, "V", 0, H)
            q_x(G)
            q_d(L, W)
            s2(L, W)
            if G + 1 < GROUPS:
                x2(G + 1)
            if G + 2 < GROUPS:
                cast(G + 2, 0, "A")
                cast(G + 2, 1, "A")


        ov = out.rearrange("(t p) h -> p t h", p=P)
        L = GROUPS - 1
        rr, o1 = {}, {}
        warm3 = keep.tile([P, 1], F32, name="warm3")

        def rsq(hh, c0, c1):
            r_t = work.tile([P, c1 - c0], F32, name="rr%d" % (c1 - c0), bufs=2)
            rr[hh, c0] = r_t
            A.activation(out=r_t[:], in_=fish[hh][:, c0:c1], func=ACT.Abs_reciprocal_sqrt, scale=1.0 / N, bias=0.2)

        def square(hh, c0, c1):
            r_t = work.tile([P, c1 - c0], F32, name="r2", bufs=1)
            A.activation(out=r_t[:], in_=rr[hh, c0][:], func=ACT.Square)
            rr[hh, c0] = r_t

        def mul1(hh, c0, c1):
            o_t = work.tile([P, c1 - c0], F32, name="o1%d" % (c1 - c0), bufs=2)
            o1[hh, c0] = o_t
            V.scalar_tensor_tensor(
                out=o_t[:], in0=grad[hh][:, c0:c1], scalar=1.0 / 64.0, in1=rr[hh, c0][:], op0=ALU.mult, op1=ALU.mult
            )

        def mul2(hh, c0, c1):
            o_t = work.tile([P, c1 - c0], F32, name="o2", bufs=2)
            V.tensor_tensor(out=o_t[:], in0=o1[hh, c0][:], in1=rr[hh, c0][:], op=ALU.mult)
            o1[hh, c0] = o_t

        def turn(hh, c0, c1, eng):
            m = (c1 - c0) // P
            xt = psum.tile([P, m, P], F32, name="xt", bufs=2)
            for d in range(m):
                PE.transpose(xt[:, d, :], o1[hh, c0][:, d * P : (d + 1) * P], ident[:])
            ot = work.tile([P, m, P], F32, name="ot%d" % m, bufs=2)
            if eng == "A":
                A.copy(out=ot[:], in_=xt[:])
            else:
                V.tensor_copy(out=ot[:], in_=xt[:])
            nc.sync.dma_start(out=ov[:, c0 // P : c1 // P, hh * P : (hh + 1) * P], in_=ot[:])

        B0, B1 = blocks(L)
        nd(L, B0)
        d2p(L, B0)
        nd(L, B1)
        d2p(L, B1)
        A.activation(out=warm3[:], in_=warm[:], func=ACT.Abs_reciprocal_sqrt)
        d_tile(L, B0)
        dq(L, B0, "V", 0, HT)
        i_d2(L, B0, "V", 0, HT)
        d_tile(L, B1)
        i_d2(L, B1, "V", 0, HT)
        q_d(L, B0)
        s2(L, B0)
        dq(L, B1, "V", 0, HT)
        a0, b0, a1, b1 = [(hh, c, c + 256) for hh in range(2) for c in (0, 256)]
        all0 = (0, 0, 512)
        rsq(*all0)
        square(*all0)
        q_d(L, B1)
        s2(L, B1)
        mul1(*all0)
        rsq(*a1)
        rsq(*b1)
        turn(*all0, "A")
        mul1(*a1)
        mul1(*b1)
        mul2(*a1)
        mul2(*b1)
        turn(*a1, "A")
        turn(*b1, "V")
